import numpy as np
import ml_dtypes


def mxq(x, axis, fmt="e4m3"):
    dtype, down = {"e4m3": (ml_dtypes.float8_e4m3fn, 7), "e5m2": (ml_dtypes.float8_e5m2, 14)}[fmt]
    v = np.moveaxis(np.asarray(x, np.float32).astype(ml_dtypes.bfloat16).astype(np.float64), axis, -1)
    blocks = v.reshape(v.shape[:-1] + (-1, 32))
    amax = np.abs(blocks).max(-1, keepdims=True)
    byte = np.maximum(np.where(amax > 0, np.frexp(amax)[1] - 1 + 127, 0) - down, 1)
    scale = np.exp2(byte - 127.0)
    codes = (blocks / scale).astype(np.float32).astype(dtype).astype(np.float64)
    return np.moveaxis((codes * scale).reshape(v.shape), -1, axis)


WIDE = False


def mx_kscale(k):
    if not WIDE:
        return np.ones(k)
    levels = np.array([10, -10, 5, -5, 0])
    if k % 512:
        return np.exp2(np.random.permutation(np.resize(levels, k // 32))).repeat(32)
    a = np.empty((k // 512, 16))
    for p in range(k // 512):
        a[p, :8] = np.random.permutation(np.resize(levels, 8))
        for g in range(8):
            far = levels[np.abs(levels - a[p, g]) >= 10]
            a[p, g + 8] = far[np.random.randint(len(far))]
    return np.exp2(a.ravel()).repeat(32)


def f64(x):
    return np.asarray(x).astype(np.float64)


def striped(idx):
    return np.tile(idx.reshape(-1, 16).T, (8, 1)).astype(np.uint16)


def unstriped(offs):
    return offs[:16].T.reshape(-1).astype(np.int64)


def striped8(idx):
    return np.concatenate([x.reshape(-1, 16).T for x in idx]).astype(np.uint16)


def runs(offs, k):
    lists = np.stack([offs[16 * r : 16 * r + 16].T.reshape(-1) for r in range(8)]).astype(np.int64)
    return lists[np.arange(k) % 512 // 64]


def pack_weight(w):
    k, n = w.shape
    w = f64(np.asarray(w, np.float32).astype(ml_dtypes.bfloat16)).reshape(k // 32, 32, n)
    amax = np.abs(w).max(1)
    byte = np.clip(np.where(amax > 0, np.frexp(amax)[1] - 1 + 127 - 7, 1), 1, 254)
    scaled = (w * np.exp2(127.0 - byte)[:, None, :]).reshape(k, n).astype(np.float32)
    words = np.ascontiguousarray(scaled.reshape(k // 512, 128, 4, n).transpose(0, 1, 3, 2)).astype(ml_dtypes.float8_e4m3fn).view(np.uint8)
    return words, np.ascontiguousarray(byte.astype(np.uint8).reshape(k // 512, 16, n))


def unpack_weight(words, scales):
    g, p, n, _ = words.shape
    vals = np.ascontiguousarray(words).view(ml_dtypes.float8_e4m3fn).astype(np.float64) * np.repeat(np.exp2(scales.astype(np.float64) - 127.0), 8, axis=1)[..., None]
    return vals.transpose(0, 1, 3, 2).reshape(g * 512, n)

def planes(y):
    n, m = y.shape
    v = y.astype(np.float32).astype(ml_dtypes.bfloat16).astype(np.float64).reshape(n // 32, 32, m)
    top = np.abs(v).max(1)
    byte = np.clip(np.where(top > 0, np.frexp(top)[1] - 1 + 127 - 7, 1), 1, 254)
    codes = (v * np.exp2(127.0 - byte)[:, None, :]).reshape(n, m).astype(np.float32).astype(ml_dtypes.float8_e4m3fn).view(np.uint8)
    words = codes.reshape(n // 512, 128, 4, m).transpose(0, 1, 3, 2)
    return np.ascontiguousarray(words), np.ascontiguousarray(byte.astype(np.uint8).reshape(n // 512, 16, m))


K, T, S, H, G = 512, 2048, 512, 512, 2048


def setup_inputs():
    n = np.random.standard_normal
    s = mx_kscale(K)[:, None]
    packed_xT = pack_weight(n((K, T)) * s)
    packed_w1 = pack_weight(n((K, H)) / np.sqrt(K) / s)
    packed_dT = pack_weight(n((K, G)) / s)
    return {
        "x_words": packed_xT[0],
        "x_scales": packed_xT[1],
        "w1_words": packed_w1[0],
        "w1_scales": packed_w1[1],
        "gs": (np.random.uniform(0.5, 1.5, (K, 1)) * s).astype(np.float32),
        "d_words": packed_dT[0],
        "d_scales": packed_dT[1],
        "offs": striped(np.random.permutation(T)[:S]),
        "n1": striped8(np.stack([np.random.permutation(S) for _ in range(8)])),
        "n2": striped8(np.stack([np.random.permutation(S) for _ in range(8)])),
        "k1": striped8(np.random.randint(0, G, (8, H))),
        "n3": striped8(np.stack([np.random.permutation(S) for _ in range(8)])),
        "n4": striped8(np.stack([np.random.permutation(S) for _ in range(8)])),
    }


def reference(x_words, x_scales, w1_words, w1_scales, gs, d_words, d_scales, offs, n1, n2, k1, n3, n4):
    d_k1 = unpack_weight(d_words, d_scales)[np.arange(K)[:, None], runs(k1, K)]
    xq = unpack_weight(x_words, x_scales)[:, unstriped(offs)]
    y = unpack_weight(w1_words, w1_scales).T @ xq
    z = f64(gs) * ((y[np.arange(H)[:, None], runs(n1, H)]) * (y[np.arange(H)[:, None], runs(n2, H)]))
    h = 0.0625 * ((d_k1.T @ mxq(z, 0, "e4m3")))
    out_0 = h - (np.minimum(h[np.arange(H)[:, None], runs(n3, H)], h[np.arange(H)[:, None], runs(n4, H)]))
    return (out_0,) + planes(out_0)

@@ -1,0 +1,228 @@
+from contextlib import ExitStack
+
+import concourse.mybir as mybir
+
+K, T, S, H, G = 512, 2048, 512, 512, 2048
+FLOPS = 2 * 2 * 512 * 512 * 512
+
+F32 = mybir.dt.float32
+BF16 = mybir.dt.bfloat16
+I32 = mybir.dt.int32
+U32 = mybir.dt.uint32
+U16 = mybir.dt.uint16
+U8 = mybir.dt.uint8
+FP8X4 = mybir.dt.float8_e4m3fn_x4
+ALU = mybir.AluOpType
+COPY = mybir.ActivationFunctionType.Copy
+
+P = 128
+PACK = 4
+LIST_ROWS = 16
+Z_CHUNKS = ((0, 384), (384, 512))
+OUT_CHUNKS = ((0, 384), (384, 512))
+
+
+def pieces(lo, hi):
+    result = []
+    while lo < hi:
+        width = 256 if hi - lo >= 256 else 128
+        result.append((lo, lo + width))
+        lo = lo + width
+    return result
+
+
+def tile_picked_denseprodunder_none_po_kernel(
+    tc, x_words, x_scales, w1_words, w1_scales, gs, d_words, d_scales, offs, n1, n2, k1, n3, n4, out_0, out_1, out_2
+):
+    nc = tc.nc
+
+    def words_of(dram):
+        return dram[0].rearrange("p n t -> p (n t)").bitcast(I32)
+
+    def entries(lists, lo, hi):
+        return lists[:, lo // LIST_ROWS : hi // LIST_ROWS]
+
+    with ExitStack() as ctx:
+        lists = ctx.enter_context(tc.tile_pool(name="lists", bufs=1))
+        pool = ctx.enter_context(tc.tile_pool(name="pool", bufs=1))
+        psum = ctx.enter_context(tc.psum_pool(name="psum", bufs=1))
+
+        def list_tile(name):
+            return lists.tile([P, S // LIST_ROWS], U16, name=name)
+
+        def sb(name, shape, dtype, tag=None):
+            return pool.tile(shape, dtype, name=name, tag=tag or name, align_bytes=64)
+
+        offs_t, k1_t = list_tile("offs_t"), list_tile("k1_t")
+        n1_t, n2_t, n3_t, n4_t = list_tile("n1_t"), list_tile("n2_t"), list_tile("n3_t"), list_tile("n4_t")
+
+        x_table = sb("x_table", [P, T], I32)
+        x_scale_table = sb("x_scale_table", [P, T], U8)
+        d_table = sb("d_table", [P, G], I32)
+        d_scale_table = sb("d_scale_table", [P, G], U8)
+        w_raw = sb("w_raw", [P, H], I32)
+        w_scale_raw = sb("w_scale_raw", [P, H], U8)
+        d_scale = sb("d_scale", [P, H], U8)
+        gain = sb("gain", [P, PACK], F32)
+
+        nc.gpsimd.memset(x_scale_table[:].bitcast(I32), 0)
+        nc.vector.memset(d_scale_table[:].bitcast(I32), 0)
+        nc.vector.memset(w_scale_raw[:].bitcast(I32), 0)
+        nc.vector.memset(d_scale[:].bitcast(I32), 0)
+
+        nc.sync.dma_start(out=w_raw[:], in_=words_of(w1_words))
+        nc.scalar.dma_start(out=x_table[:], in_=words_of(x_words))
+        nc.sync.dma_start(offs_t[:], offs)
+        for q in range(4):
+            nc.sync.dma_start(
+                out=x_scale_table[32 * q : 32 * q + 4, :].bitcast(I32),
+                in_=x_scales[0, 4 * q : 4 * q + 4, :].bitcast(I32),
+            )
+        nc.sync.dma_start(out=d_scale_table[0:P:8, :].bitcast(I32), in_=d_scales[0].bitcast(I32))
+        nc.sync.dma_start(k1_t[:], k1)
+        for q in range(4):
+            nc.sync.dma_start(
+                out=w_scale_raw[32 * q : 32 * q + 4, :].bitcast(I32),
+                in_=w1_scales[0, 4 * q : 4 * q + 4, :].bitcast(I32),
+            )
+        nc.gpsimd.dma_start(out=gain[:], in_=gs.rearrange("(p t) o -> p (t o)", t=PACK))
+        nc.sync.dma_start(out=d_table[:], in_=words_of(d_words))
+        nc.sync.dma_start(n1_t[:], n1)
+        nc.sync.dma_start(n2_t[:], n2)
+        nc.sync.dma_start(n3_t[:], n3)
+        nc.sync.dma_start(n4_t[:], n4)
+
+        def deal(dst, src):
+            nc.vector.tensor_copy(
+                out=dst[:].rearrange("p (t m) -> p t m", t=PACK), in_=src[:].rearrange("p (m t) -> p t m", t=PACK)
+            )
+
+        x_scale = sb("x_scale", [P, S], U8)
+        x_codes = sb("x_codes", [P, S], I32)
+        w_codes = sb("w_codes", [P, H], I32)
+        w_scale = sb("w_scale", [P, H], U8)
+        nc.vector.tensor_copy(x_scale[:], x_scale_table[:].indirect(offs_t[:]))
+        deal(w_codes, w_raw)
+        nc.vector.tensor_copy(x_codes[:].bitcast(U32), x_table[:].bitcast(U32).indirect(offs_t[:]))
+        d_scale_picked = sb("d_scale_picked", [P, H], U8)
+        nc.vector.tensor_copy(d_scale_picked[:], d_scale_table[:].indirect(k1_t[:]))
+        deal(w_scale, w_scale_raw)
+
+        y_banks = [psum.tile([P, S], F32, name="y_bank%d" % t) for t in range(PACK)]
+        y_plain = [sb("y_plain%d" % t, [P, S], F32) for t in range(PACK)]
+        y_gain = [sb("y_gain%d" % t, [P, S], F32) for t in range(PACK)]
+        for t in range(PACK):
+            cols = slice(t * P, (t + 1) * P)
+            nc.tensor.matmul_mx(
+                out=y_banks[t][:],
+                lhsT=w_codes[:, cols].bitcast(FP8X4),
+                lhsT_scale=w_scale[:, cols],
+                rhs=x_codes[:].bitcast(FP8X4),
+                rhs_scale=x_scale[:],
+                start=True,
+                stop=True,
+            )
+            nc.scalar.activation(y_gain[t][:], y_banks[t][:], COPY, scale=gain[:, t : t + 1])
+            nc.scalar.activation(y_plain[t][:], y_banks[t][:], COPY)
+
+        d_scale_dealt = sb("d_scale_dealt", [P, H], U8)
+        d_picked = sb("d_picked", [P, H], I32, tag="w_scale_raw")
+        d_codes = sb("d_codes", [P, H], I32)
+        nc.vector.tensor_copy(d_picked[:].bitcast(U32), d_table[:].bitcast(U32).indirect(k1_t[:]))
+        deal(d_scale_dealt, d_scale_picked)
+        deal(d_codes, d_picked)
+        for q in range(4):
+            nc.sync.dma_start(
+                out=d_scale[32 * q : 32 * q + 4, :].bitcast(I32),
+                in_=d_scale_dealt[32 * q : 32 * q + 32 : 8, :].bitcast(I32),
+            )
+
+        def interleave(name, planes, width):
+            grouped = sb(name, [P, width, PACK], BF16)
+            nc.scalar.copy(
+                out=grouped[:].rearrange("p (c i) t -> p c t i", i=4),
+                in_=planes[:].rearrange("p t (c i) -> p c t i", i=4),
+            )
+            return grouped
+
+        def quantize(grouped, base, lo, hi, codes, scale):
+            nc.vector.quantize_mx(
+                out=codes[:, lo:hi].bitcast(FP8X4),
+                scales=scale[:, lo:hi],
+                in_=grouped[:, lo - base : hi - base, :].rearrange("p c t -> p (c t)"),
+            )
+
+        z_grouped = []
+        for lo, hi in Z_CHUNKS:
+            width = hi - lo
+            first = sb("z_first%d" % lo, [P, PACK, width], F32)
+            z = sb("z%d" % lo, [P, PACK, width], F32)
+            for t in range(PACK + 1):
+                if t < PACK:
+                    nc.vector.tensor_copy(first[:, t, :], y_gain[t][:].indirect(entries(n1_t, lo, hi)))
+                if t > 0:
+                    nc.vector.tensor_tensor(
+                        z[:, t - 1, :], y_plain[t - 1][:].indirect(entries(n2_t, lo, hi)), first[:, t - 1, :], ALU.mult
+                    )
+            z_grouped.append(interleave("z_grouped%d" % lo, z, width))
+
+        z_codes = sb("z_codes", [P, S], I32)
+        z_scale = sb("z_scale", [P, S], U8)
+        h = [sb("h%d" % t, [P, S], F32) for t in range(PACK)]
+        for (base, end), grouped in zip(Z_CHUNKS, z_grouped):
+            for lo, hi in pieces(base, end):
+                quantize(grouped, base, lo, hi, z_codes, z_scale)
+
+        def second_product(name, t, base, end, spans):
+            bank = psum.tile([P, S], F32, name=name)
+            cols = slice(t * P, (t + 1) * P)
+            for lo, hi in spans:
+                nc.tensor.matmul_mx(
+                    out=bank[:, lo:hi],
+                    lhsT=d_codes[:, cols].bitcast(FP8X4),
+                    lhsT_scale=d_scale[:, cols],
+                    rhs=z_codes[:, lo:hi].bitcast(FP8X4),
+                    rhs_scale=z_scale[:, lo:hi],
+                    start=True,
+                    stop=True,
+                )
+            nc.scalar.activation(h[t][:, base:end], bank[:, base:end], COPY, scale=0.0625)
+
+        second_product("h_bank0", 0, 0, 384, pieces(0, 384))
+        second_product("h_bank1", 0, 384, 512, pieces(384, 512))
+        second_product("h_bank2", 1, 0, S, [(0, S)])
+        second_product("h_bank3", 2, 0, S, [(0, S)])
+        second_product("y_bank0", 3, 0, S, [(0, S)])
+
+        out_rows = out_0.rearrange("(p t) j -> p t j", t=PACK)
+        out_codes = sb("out_codes", [P, S], I32)
+        out_scale = sb("out_scale", [P, S], U8)
+        out_words = words_of(out_1)
+        out_grouped = []
+        for lo, hi in OUT_CHUNKS:
+            width = hi - lo
+            at3 = sb("at3_%d" % lo, [P, PACK, width], F32)
+            at4 = sb("at4_%d" % lo, [P, PACK, width], F32)
+            least = sb("least%d" % lo, [P, PACK, width], F32)
+            result = sb("result%d" % lo, [P, PACK, width], F32)
+            for t in range(PACK + 2):
+                if t < PACK:
+                    nc.vector.tensor_copy(at3[:, t, :], h[t][:].indirect(entries(n3_t, lo, hi)))
+                if 2 <= t:
+                    nc.vector.tensor_tensor(result[:, t - 2, :], h[t - 2][:, lo:hi], least[:, t - 2, :], ALU.subtract)
+                    nc.sync.dma_start(out=out_rows[:, t - 2, lo:hi], in_=result[:, t - 2, :])
+                if 1 <= t <= PACK:
+                    nc.vector.tensor_tensor(least[:, t - 1, :], at3[:, t - 1, :], at4[:, t - 1, :], ALU.min)
+                if t < PACK:
+                    nc.vector.tensor_copy(at4[:, t, :], h[t][:].indirect(entries(n4_t, lo, hi)))
+            out_grouped.append(interleave("out_grouped%d" % lo, result, width))
+
+        for (base, end), grouped in zip(OUT_CHUNKS, out_grouped):
+            for lo, hi in pieces(base, end):
+                quantize(grouped, base, lo, hi, out_codes, out_scale)
+            nc.sync.dma_start(out=out_words[:, base:end], in_=out_codes[:, base:end])
+        for q in range(4):
+            queue = nc.sync if q % 2 == 0 else nc.scalar
+            queue.dma_start(
+                out=out_2[0, 4 * q : 4 * q + 4, :].bitcast(I32), in_=out_scale[32 * q : 32 * q + 4, :].bitcast(I32)
+            )

@@ -58,39 +58,30 @@ def tile_picked_denseprodunder_none_po_kernel(
 
         x_table = sb("x_table", [P, T], I32)
         x_scale_table = sb("x_scale_table", [P, T], U8)
-        d_table = sb("d_table", [P, G], I32)
         d_scale_table = sb("d_scale_table", [P, G], U8)
         w_raw = sb("w_raw", [P, H], I32)
         w_scale_raw = sb("w_scale_raw", [P, H], U8)
         d_scale = sb("d_scale", [P, H], U8)
         gain = sb("gain", [P, PACK], F32)
 
-        nc.gpsimd.memset(x_scale_table[:].bitcast(I32), 0)
+        nc.vector.memset(x_scale_table[:].bitcast(I32), 0)
+        nc.gpsimd.memset(w_scale_raw[:].bitcast(I32), 0)
         nc.vector.memset(d_scale_table[:].bitcast(I32), 0)
-        nc.vector.memset(w_scale_raw[:].bitcast(I32), 0)
-        nc.vector.memset(d_scale[:].bitcast(I32), 0)
 
+        def load_scale_rows(queue, tile, dram):
+            for q in range(4):
+                queue.dma_start(
+                    out=tile[32 * q : 32 * q + 4, :].bitcast(I32), in_=dram[0, 4 * q : 4 * q + 4, :].bitcast(I32)
+                )
+
+        for tile, dram in ((offs_t, offs), (k1_t, k1), (n1_t, n1), (n2_t, n2), (n3_t, n3), (n4_t, n4)):
+            nc.sync.dma_start(tile[:], dram)
+        nc.sync.dma_start(out=x_table[:], in_=words_of(x_words))
         nc.sync.dma_start(out=w_raw[:], in_=words_of(w1_words))
-        nc.scalar.dma_start(out=x_table[:], in_=words_of(x_words))
-        nc.sync.dma_start(offs_t[:], offs)
-        for q in range(4):
-            nc.sync.dma_start(
-                out=x_scale_table[32 * q : 32 * q + 4, :].bitcast(I32),
-                in_=x_scales[0, 4 * q : 4 * q + 4, :].bitcast(I32),
-            )
-        nc.sync.dma_start(out=d_scale_table[0:P:8, :].bitcast(I32), in_=d_scales[0].bitcast(I32))
-        nc.sync.dma_start(k1_t[:], k1)
-        for q in range(4):
-            nc.sync.dma_start(
-                out=w_scale_raw[32 * q : 32 * q + 4, :].bitcast(I32),
-                in_=w1_scales[0, 4 * q : 4 * q + 4, :].bitcast(I32),
-            )
-        nc.gpsimd.dma_start(out=gain[:], in_=gs.rearrange("(p t) o -> p (t o)", t=PACK))
-        nc.sync.dma_start(out=d_table[:], in_=words_of(d_words))
-        nc.sync.dma_start(n1_t[:], n1)
-        nc.sync.dma_start(n2_t[:], n2)
-        nc.sync.dma_start(n3_t[:], n3)
-        nc.sync.dma_start(n4_t[:], n4)
+        nc.sync.dma_start(out=gain[:], in_=gs.rearrange("(p t) o -> p (t o)", t=PACK))
+        load_scale_rows(nc.scalar, x_scale_table, x_scales)
+        load_scale_rows(nc.gpsimd, w_scale_raw, w1_scales)
+        nc.scalar.dma_start(out=d_scale_table[0:P:8, :].bitcast(I32), in_=d_scales[0].bitcast(I32))
 
         def deal(dst, src):
             nc.vector.tensor_copy(
@@ -102,10 +93,10 @@ def tile_picked_denseprodunder_none_po_kernel(
         w_codes = sb("w_codes", [P, H], I32)
         w_scale = sb("w_scale", [P, H], U8)
         nc.vector.tensor_copy(x_scale[:], x_scale_table[:].indirect(offs_t[:]))
-        deal(w_codes, w_raw)
+        d_table = sb("d_table", [P, G], I32, tag="x_scale_table")
+        nc.sync.dma_start(out=d_table[:], in_=words_of(d_words))
         nc.vector.tensor_copy(x_codes[:].bitcast(U32), x_table[:].bitcast(U32).indirect(offs_t[:]))
-        d_scale_picked = sb("d_scale_picked", [P, H], U8)
-        nc.vector.tensor_copy(d_scale_picked[:], d_scale_table[:].indirect(k1_t[:]))
+        deal(w_codes, w_raw)
         deal(w_scale, w_scale_raw)
 
         y_banks = [psum.tile([P, S], F32, name="y_bank%d" % t) for t in range(PACK)]
@@ -125,11 +116,13 @@ def tile_picked_denseprodunder_none_po_kernel(
             nc.scalar.activation(y_gain[t][:], y_banks[t][:], COPY, scale=gain[:, t : t + 1])
             nc.scalar.activation(y_plain[t][:], y_banks[t][:], COPY)
 
+        d_scale_picked = sb("d_scale_picked", [P, H], U8, tag="w_scale_raw")
         d_scale_dealt = sb("d_scale_dealt", [P, H], U8)
-        d_picked = sb("d_picked", [P, H], I32, tag="w_scale_raw")
+        d_picked = sb("d_picked", [P, H], I32)
         d_codes = sb("d_codes", [P, H], I32)
-        nc.vector.tensor_copy(d_picked[:].bitcast(U32), d_table[:].bitcast(U32).indirect(k1_t[:]))
+        nc.vector.tensor_copy(d_scale_picked[:], d_scale_table[:].indirect(k1_t[:]))
         deal(d_scale_dealt, d_scale_picked)
+        nc.vector.tensor_copy(d_picked[:].bitcast(U32), d_table[:].bitcast(U32).indirect(k1_t[:]))
         deal(d_codes, d_picked)
         for q in range(4):
             nc.sync.dma_start(

@@ -19,7 +19,7 @@ P = 128
 PACK = 4
 LIST_ROWS = 16
 Z_CHUNKS = ((0, 384), (384, 512))
-OUT_CHUNKS = ((0, 384), (384, 512))
+OUT_CHUNKS = ((0, 256), (256, 384), (384, 512))
 
 
 def pieces(lo, hi):
@@ -68,24 +68,25 @@ def tile_picked_denseprodunder_none_po_kernel(
         nc.gpsimd.memset(w_scale_raw[:].bitcast(I32), 0)
         nc.vector.memset(d_scale_table[:].bitcast(I32), 0)
 
-        def load_scale_rows(queue, tile, dram):
-            for q in range(4):
+        def load_scale_rows(queues, tile, dram):
+            for q, queue in enumerate(queues):
                 queue.dma_start(
                     out=tile[32 * q : 32 * q + 4, :].bitcast(I32), in_=dram[0, 4 * q : 4 * q + 4, :].bitcast(I32)
                 )
 
-        for tile, dram in ((offs_t, offs), (k1_t, k1), (n1_t, n1), (n2_t, n2), (n3_t, n3), (n4_t, n4)):
-            nc.sync.dma_start(tile[:], dram)
+        nc.sync.dma_start(offs_t[:], offs)
         nc.sync.dma_start(out=x_table[:], in_=words_of(x_words))
-        nc.sync.dma_start(out=w_raw[:], in_=words_of(w1_words))
-        nc.sync.dma_start(out=gain[:], in_=gs.rearrange("(p t) o -> p (t o)", t=PACK))
-        load_scale_rows(nc.scalar, x_scale_table, x_scales)
-        load_scale_rows(nc.gpsimd, w_scale_raw, w1_scales)
-        nc.scalar.dma_start(out=d_scale_table[0:P:8, :].bitcast(I32), in_=d_scales[0].bitcast(I32))
+        nc.scalar.dma_start(out=w_raw[:], in_=words_of(w1_words))
+        load_scale_rows([nc.scalar] * 4, x_scale_table, x_scales)
+        load_scale_rows([nc.gpsimd] + [nc.scalar] * 3, w_scale_raw, w1_scales)
+        nc.gpsimd.dma_start(out=gain[:], in_=gs.rearrange("(p t) o -> p (t o)", t=PACK))
+        nc.sync.dma_start(out=d_scale_table[0:P:8, :].bitcast(I32), in_=d_scales[0].bitcast(I32))
+        for tile, dram in ((k1_t, k1), (n1_t, n1), (n2_t, n2), (n3_t, n3), (n4_t, n4)):
+            nc.sync.dma_start(tile[:], dram)
 
         def deal(dst, src):
             nc.vector.tensor_copy(
-                out=dst[:].rearrange("p (t m) -> p t m", t=PACK), in_=src[:].rearrange("p (m t) -> p t m", t=PACK)
+                out=dst[:].rearrange("p (t m) -> p m t", t=PACK), in_=src[:].rearrange("p (m t) -> p m t", t=PACK)
             )
 
         x_scale = sb("x_scale", [P, S], U8)
@@ -162,6 +163,7 @@ def tile_picked_denseprodunder_none_po_kernel(
         z_codes = sb("z_codes", [P, S], I32)
         z_scale = sb("z_scale", [P, S], U8)
         h = [sb("h%d" % t, [P, S], F32) for t in range(PACK)]
+        h_neg = [sb("h_neg%d" % t, [P, S], F32) for t in range(PACK)]
         for (base, end), grouped in zip(Z_CHUNKS, z_grouped):
             for lo, hi in pieces(base, end):
                 quantize(grouped, base, lo, hi, z_codes, z_scale)
@@ -179,6 +181,7 @@ def tile_picked_denseprodunder_none_po_kernel(
                     start=True,
                     stop=True,
                 )
+            nc.scalar.activation(h_neg[t][:, base:end], bank[:, base:end], COPY, scale=-0.0625)
             nc.scalar.activation(h[t][:, base:end], bank[:, base:end], COPY, scale=0.0625)
 
         second_product("h_bank0", 0, 0, 384, pieces(0, 384))
@@ -194,20 +197,22 @@ def tile_picked_denseprodunder_none_po_kernel(
         out_grouped = []
         for lo, hi in OUT_CHUNKS:
             width = hi - lo
-            at3 = sb("at3_%d" % lo, [P, PACK, width], F32)
-            at4 = sb("at4_%d" % lo, [P, PACK, width], F32)
-            least = sb("least%d" % lo, [P, PACK, width], F32)
+            above3 = sb("above3_%d" % lo, [P, PACK, width], F32)
+            above4 = sb("above4_%d" % lo, [P, PACK, width], F32)
             result = sb("result%d" % lo, [P, PACK, width], F32)
-            for t in range(PACK + 2):
+            for t in range(PACK + 1):
                 if t < PACK:
-                    nc.vector.tensor_copy(at3[:, t, :], h[t][:].indirect(entries(n3_t, lo, hi)))
-                if 2 <= t:
-                    nc.vector.tensor_tensor(result[:, t - 2, :], h[t - 2][:, lo:hi], least[:, t - 2, :], ALU.subtract)
-                    nc.sync.dma_start(out=out_rows[:, t - 2, lo:hi], in_=result[:, t - 2, :])
-                if 1 <= t <= PACK:
-                    nc.vector.tensor_tensor(least[:, t - 1, :], at3[:, t - 1, :], at4[:, t - 1, :], ALU.min)
+                    nc.vector.tensor_tensor(
+                        above3[:, t, :], h_neg[t][:].indirect(entries(n3_t, lo, hi)), h[t][:, lo:hi], ALU.add
+                    )
+                if t > 0 and t % 2 == 0:
+                    pair = slice(t - 2, t)
+                    nc.vector.tensor_tensor(result[:, pair, :], above3[:, pair, :], above4[:, pair, :], ALU.max)
+                    nc.sync.dma_start(out=out_rows[:, pair, lo:hi], in_=result[:, pair, :])
                 if t < PACK:
-                    nc.vector.tensor_copy(at4[:, t, :], h[t][:].indirect(entries(n4_t, lo, hi)))
+                    nc.vector.tensor_tensor(
+                        above4[:, t, :], h_neg[t][:].indirect(entries(n4_t, lo, hi)), h[t][:, lo:hi], ALU.add
+                    )
             out_grouped.append(interleave("out_grouped%d" % lo, result, width))
 
         for (base, end), grouped in zip(OUT_CHUNKS, out_grouped):

@@ -2,7 +2,7 @@ from contextlib import ExitStack
 
 import concourse.mybir as mybir
 
-K, T, S, H, G = 512, 2048, 512, 512, 2048
+T, S, H, G = 2048, 512, 512, 2048
 FLOPS = 2 * 2 * 512 * 512 * 512
 
 F32 = mybir.dt.float32
@@ -18,17 +18,12 @@ COPY = mybir.ActivationFunctionType.Copy
 P = 128
 PACK = 4
 LIST_ROWS = 16
-Z_CHUNKS = ((0, 384), (384, 512))
-OUT_CHUNKS = ((0, 256), (256, 384), (384, 512))
-
-
-def pieces(lo, hi):
-    result = []
-    while lo < hi:
-        width = 256 if hi - lo >= 256 else 128
-        result.append((lo, lo + width))
-        lo = lo + width
-    return result
+H_SCALE = 0.0625
+SPLIT = 384
+HALF = S // 2
+Z_PARTS = ((0, SPLIT), (SPLIT, S))
+OUT_PARTS = ((0, HALF), (HALF, SPLIT), (SPLIT, S))
+QUANT_SPANS = ((0, HALF), (HALF, SPLIT), (SPLIT, S))
 
 
 def tile_picked_denseprodunder_none_po_kernel(
@@ -39,46 +34,47 @@ def tile_picked_denseprodunder_none_po_kernel(
     def words_of(dram):
         return dram[0].rearrange("p n t -> p (n t)").bitcast(I32)
 
-    def entries(lists, lo, hi):
-        return lists[:, lo // LIST_ROWS : hi // LIST_ROWS]
+    def entries(list_tile, lo, hi):
+        return list_tile[:, lo // LIST_ROWS : hi // LIST_ROWS]
 
     with ExitStack() as ctx:
         lists = ctx.enter_context(tc.tile_pool(name="lists", bufs=1))
         pool = ctx.enter_context(tc.tile_pool(name="pool", bufs=1))
         psum = ctx.enter_context(tc.psum_pool(name="psum", bufs=1))
 
-        def list_tile(name):
-            return lists.tile([P, S // LIST_ROWS], U16, name=name)
-
         def sb(name, shape, dtype, tag=None):
             return pool.tile(shape, dtype, name=name, tag=tag or name, align_bytes=64)
 
-        offs_t, k1_t = list_tile("offs_t"), list_tile("k1_t")
-        n1_t, n2_t, n3_t, n4_t = list_tile("n1_t"), list_tile("n2_t"), list_tile("n3_t"), list_tile("n4_t")
+        offs_t, k1_t, n1_t, n2_t, n3_t, n4_t = [
+            lists.tile([P, S // LIST_ROWS], U16, name=name) for name in ("offs_t", "k1_t", "n1_t", "n2_t", "n3_t", "n4_t")
+        ]
 
         x_table = sb("x_table", [P, T], I32)
         x_scale_table = sb("x_scale_table", [P, T], U8)
         d_scale_table = sb("d_scale_table", [P, G], U8)
         w_raw = sb("w_raw", [P, H], I32)
         w_scale_raw = sb("w_scale_raw", [P, H], U8)
-        d_scale = sb("d_scale", [P, H], U8)
         gain = sb("gain", [P, PACK], F32)
+        wide = [sb("wide%d" % i, [P, 2 * S], F32) for i in range(PACK)]
 
-        nc.vector.memset(x_scale_table[:].bitcast(I32), 0)
-        nc.gpsimd.memset(w_scale_raw[:].bitcast(I32), 0)
+        nc.vector.memset(x_scale_table[:, 0 : T // 2].bitcast(I32), 0)
+        nc.gpsimd.memset(x_scale_table[:, T // 2 : T].bitcast(I32), 0)
+        nc.vector.memset(w_scale_raw[:].bitcast(I32), 0)
         nc.vector.memset(d_scale_table[:].bitcast(I32), 0)
+        for window in wide:
+            nc.vector.memset(window[:, S:], 0.0)
 
-        def load_scale_rows(queues, tile, dram):
-            for q, queue in enumerate(queues):
-                queue.dma_start(
+        def load_scale_rows(tile, dram):
+            for q in range(4):
+                nc.sync.dma_start(
                     out=tile[32 * q : 32 * q + 4, :].bitcast(I32), in_=dram[0, 4 * q : 4 * q + 4, :].bitcast(I32)
                 )
 
         nc.sync.dma_start(offs_t[:], offs)
         nc.sync.dma_start(out=x_table[:], in_=words_of(x_words))
-        nc.scalar.dma_start(out=w_raw[:], in_=words_of(w1_words))
-        load_scale_rows([nc.scalar] * 4, x_scale_table, x_scales)
-        load_scale_rows([nc.gpsimd] + [nc.scalar] * 3, w_scale_raw, w1_scales)
+        nc.sync.dma_start(out=w_raw[:], in_=words_of(w1_words))
+        load_scale_rows(x_scale_table, x_scales)
+        load_scale_rows(w_scale_raw, w1_scales)
         nc.gpsimd.dma_start(out=gain[:], in_=gs.rearrange("(p t) o -> p (t o)", t=PACK))
         nc.sync.dma_start(out=d_scale_table[0:P:8, :].bitcast(I32), in_=d_scales[0].bitcast(I32))
         for tile, dram in ((k1_t, k1), (n1_t, n1), (n2_t, n2), (n3_t, n3), (n4_t, n4)):
@@ -100,25 +96,29 @@ def tile_picked_denseprodunder_none_po_kernel(
         deal(w_codes, w_raw)
         deal(w_scale, w_scale_raw)
 
-        y_banks = [psum.tile([P, S], F32, name="y_bank%d" % t) for t in range(PACK)]
-        y_plain = [sb("y_plain%d" % t, [P, S], F32) for t in range(PACK)]
-        y_gain = [sb("y_gain%d" % t, [P, S], F32) for t in range(PACK)]
-        for t in range(PACK):
+        def product(bank, codes, scale, t, moving, moving_scale, lo, hi):
             cols = slice(t * P, (t + 1) * P)
             nc.tensor.matmul_mx(
-                out=y_banks[t][:],
-                lhsT=w_codes[:, cols].bitcast(FP8X4),
-                lhsT_scale=w_scale[:, cols],
-                rhs=x_codes[:].bitcast(FP8X4),
-                rhs_scale=x_scale[:],
+                out=bank[:, lo:hi],
+                lhsT=codes[:, cols].bitcast(FP8X4),
+                lhsT_scale=scale[:, cols],
+                rhs=moving[:, lo:hi].bitcast(FP8X4),
+                rhs_scale=moving_scale[:, lo:hi],
                 start=True,
                 stop=True,
             )
-            nc.scalar.activation(y_gain[t][:], y_banks[t][:], COPY, scale=gain[:, t : t + 1])
-            nc.scalar.activation(y_plain[t][:], y_banks[t][:], COPY)
+
+        y_gain = wide[0:2] + [sb("y_gain%d" % t, [P, S], F32) for t in (2, 3)]
+        y_plain = wide[2:4] + [sb("y_plain%d" % t, [P, S], F32) for t in (2, 3)]
+        for t in range(PACK):
+            bank = psum.tile([P, S], F32, name="y_bank%d" % t)
+            product(bank, w_codes, w_scale, t, x_codes, x_scale, 0, S)
+            nc.scalar.activation(y_gain[t][:, 0:S], bank[:], COPY, scale=gain[:, t : t + 1])
+            nc.scalar.activation(y_plain[t][:, 0:S], bank[:], COPY)
 
         d_scale_picked = sb("d_scale_picked", [P, H], U8, tag="w_scale_raw")
         d_scale_dealt = sb("d_scale_dealt", [P, H], U8)
+        d_scale = sb("d_scale", [P, H], U8)
         d_picked = sb("d_picked", [P, H], I32)
         d_codes = sb("d_codes", [P, H], I32)
         nc.vector.tensor_copy(d_scale_picked[:], d_scale_table[:].indirect(k1_t[:]))
@@ -131,94 +131,89 @@ def tile_picked_denseprodunder_none_po_kernel(
                 in_=d_scale_dealt[32 * q : 32 * q + 32 : 8, :].bitcast(I32),
             )
 
-        def interleave(name, planes, width):
-            grouped = sb(name, [P, width, PACK], BF16)
-            nc.scalar.copy(
-                out=grouped[:].rearrange("p (c i) t -> p c t i", i=4),
-                in_=planes[:].rearrange("p t (c i) -> p c t i", i=4),
-            )
-            return grouped
+        def interleave(grouped, first_t, pair_columns):
+            nc.scalar.copy(out=grouped[:, :, first_t : first_t + 2], in_=pair_columns.rearrange("p t c -> p c t"))
 
-        def quantize(grouped, base, lo, hi, codes, scale):
-            nc.vector.quantize_mx(
-                out=codes[:, lo:hi].bitcast(FP8X4),
-                scales=scale[:, lo:hi],
-                in_=grouped[:, lo - base : hi - base, :].rearrange("p c t -> p (c t)"),
-            )
-
-        z_grouped = []
-        for lo, hi in Z_CHUNKS:
-            width = hi - lo
-            first = sb("z_first%d" % lo, [P, PACK, width], F32)
-            z = sb("z%d" % lo, [P, PACK, width], F32)
-            for t in range(PACK + 1):
-                if t < PACK:
-                    nc.vector.tensor_copy(first[:, t, :], y_gain[t][:].indirect(entries(n1_t, lo, hi)))
-                if t > 0:
-                    nc.vector.tensor_tensor(
-                        z[:, t - 1, :], y_plain[t - 1][:].indirect(entries(n2_t, lo, hi)), first[:, t - 1, :], ALU.mult
+        def quantize(grouped, base, end, codes, scale):
+            for lo, hi in QUANT_SPANS:
+                if base <= lo and hi <= end:
+                    nc.vector.quantize_mx(
+                        out=codes[:, lo:hi].bitcast(FP8X4),
+                        scales=scale[:, lo:hi],
+                        in_=grouped[:, lo - base : hi - base, :].rearrange("p c t -> p (c t)"),
                     )
-            z_grouped.append(interleave("z_grouped%d" % lo, z, width))
+
+        def steps(parts):
+            return [(0, 0, S)] + [(2, lo, hi) for lo, hi in parts]
+
+        def interleave_step(grouped, parts, first_t, lo, hi, pair):
+            for tile, (part_lo, part_hi) in zip(grouped, parts):
+                if lo <= part_lo and part_hi <= hi:
+                    interleave(tile, first_t, pair[:, :, part_lo - lo : part_hi - lo])
+
+        z_grouped = [sb("z_grouped%d" % lo, [P, hi - lo, PACK], BF16) for lo, hi in Z_PARTS]
+        for first_t, lo, hi in steps(Z_PARTS):
+            at_n1 = sb("at_n1_%d_%d" % (first_t, lo), [P, 2, hi - lo], F32)
+            z = sb("z_%d_%d" % (first_t, lo), [P, 2, hi - lo], F32)
+            for i in range(2):
+                nc.vector.tensor_copy(at_n1[:, i, :], y_gain[first_t + i][:].indirect(entries(n1_t, lo, hi)))
+            for i in range(2):
+                nc.vector.tensor_tensor(
+                    z[:, i, :], y_plain[first_t + i][:].indirect(entries(n2_t, lo, hi)), at_n1[:, i, :], ALU.mult
+                )
+            interleave_step(z_grouped, Z_PARTS, first_t, lo, hi, z)
 
         z_codes = sb("z_codes", [P, S], I32)
         z_scale = sb("z_scale", [P, S], U8)
+        for grouped, (lo, hi) in zip(z_grouped, Z_PARTS):
+            quantize(grouped, lo, hi, z_codes, z_scale)
+
+        h_neg = y_gain
         h = [sb("h%d" % t, [P, S], F32) for t in range(PACK)]
-        h_neg = [sb("h_neg%d" % t, [P, S], F32) for t in range(PACK)]
-        for (base, end), grouped in zip(Z_CHUNKS, z_grouped):
-            for lo, hi in pieces(base, end):
-                quantize(grouped, base, lo, hi, z_codes, z_scale)
-
-        def second_product(name, t, base, end, spans):
-            bank = psum.tile([P, S], F32, name=name)
-            cols = slice(t * P, (t + 1) * P)
-            for lo, hi in spans:
-                nc.tensor.matmul_mx(
-                    out=bank[:, lo:hi],
-                    lhsT=d_codes[:, cols].bitcast(FP8X4),
-                    lhsT_scale=d_scale[:, cols],
-                    rhs=z_codes[:, lo:hi].bitcast(FP8X4),
-                    rhs_scale=z_scale[:, lo:hi],
-                    start=True,
-                    stop=True,
-                )
-            nc.scalar.activation(h_neg[t][:, base:end], bank[:, base:end], COPY, scale=-0.0625)
-            nc.scalar.activation(h[t][:, base:end], bank[:, base:end], COPY, scale=0.0625)
-
-        second_product("h_bank0", 0, 0, 384, pieces(0, 384))
-        second_product("h_bank1", 0, 384, 512, pieces(384, 512))
-        second_product("h_bank2", 1, 0, S, [(0, S)])
-        second_product("h_bank3", 2, 0, S, [(0, S)])
-        second_product("y_bank0", 3, 0, S, [(0, S)])
+        left = psum.tile([P, S], F32, name="h_left")
+        right = psum.tile([P, S], F32, name="h_right")
+        product(left, d_codes, d_scale, 0, z_codes, z_scale, 0, HALF)
+        product(right, d_codes, d_scale, 0, z_codes, z_scale, HALF, S)
+        nc.scalar.activation(h_neg[0][:, 0:HALF], left[:, 0:HALF], COPY, scale=-H_SCALE)
+        nc.scalar.activation(h[0][:, 0:HALF], left[:, 0:HALF], COPY, scale=H_SCALE)
+        nc.vector.tensor_scalar(h_neg[0][:, HALF:S], right[:, HALF:S], -H_SCALE, None, ALU.mult)
+        nc.scalar.activation(h[0][:, HALF:S], right[:, HALF:S], COPY, scale=H_SCALE)
+        for t in range(1, PACK):
+            bank = psum.tile([P, S], F32, name="y_bank%d" % t)
+            product(bank, d_codes, d_scale, t, z_codes, z_scale, 0, S)
+            nc.scalar.activation(h_neg[t][:, 0:S], bank[:], COPY, scale=-H_SCALE)
+            nc.scalar.activation(h[t][:], bank[:], COPY, scale=H_SCALE)
 
         out_rows = out_0.rearrange("(p t) j -> p t j", t=PACK)
+        out_grouped = [sb("out_grouped%d" % lo, [P, hi - lo, PACK], BF16) for lo, hi in OUT_PARTS]
+
+        def above(dst, t, list_tile, lo, hi):
+            nc.vector.tensor_tensor(dst, h_neg[t][:].indirect(entries(list_tile, lo, hi)), h[t][:, lo:hi], ALU.add)
+
+        def finish(first_t, lo, hi, above3, above4):
+            result = sb("result_%d_%d" % (first_t, lo), [P, 2, hi - lo], F32)
+            nc.vector.tensor_tensor(result[:], above3[:], above4[:], ALU.max)
+            nc.sync.dma_start(out=out_rows[:, first_t : first_t + 2, lo:hi], in_=result[:])
+            interleave_step(out_grouped, OUT_PARTS, first_t, lo, hi, result)
+
+        pending = None
+        for first_t, lo, hi in steps(OUT_PARTS):
+            above3 = sb("above3_%d_%d" % (first_t, lo), [P, 2, hi - lo], F32)
+            above4 = sb("above4_%d_%d" % (first_t, lo), [P, 2, hi - lo], F32)
+            above(above3[:, 0, :], first_t, n3_t, lo, hi)
+            if pending:
+                finish(*pending)
+            above(above4[:, 0, :], first_t, n4_t, lo, hi)
+            above(above3[:, 1, :], first_t + 1, n3_t, lo, hi)
+            above(above4[:, 1, :], first_t + 1, n4_t, lo, hi)
+            pending = (first_t, lo, hi, above3, above4)
+        finish(*pending)
+
         out_codes = sb("out_codes", [P, S], I32)
         out_scale = sb("out_scale", [P, S], U8)
-        out_words = words_of(out_1)
-        out_grouped = []
-        for lo, hi in OUT_CHUNKS:
-            width = hi - lo
-            above3 = sb("above3_%d" % lo, [P, PACK, width], F32)
-            above4 = sb("above4_%d" % lo, [P, PACK, width], F32)
-            result = sb("result%d" % lo, [P, PACK, width], F32)
-            for t in range(PACK + 1):
-                if t < PACK:
-                    nc.vector.tensor_tensor(
-                        above3[:, t, :], h_neg[t][:].indirect(entries(n3_t, lo, hi)), h[t][:, lo:hi], ALU.add
-                    )
-                if t > 0 and t % 2 == 0:
-                    pair = slice(t - 2, t)
-                    nc.vector.tensor_tensor(result[:, pair, :], above3[:, pair, :], above4[:, pair, :], ALU.max)
-                    nc.sync.dma_start(out=out_rows[:, pair, lo:hi], in_=result[:, pair, :])
-                if t < PACK:
-                    nc.vector.tensor_tensor(
-                        above4[:, t, :], h_neg[t][:].indirect(entries(n4_t, lo, hi)), h[t][:, lo:hi], ALU.add
-                    )
-            out_grouped.append(interleave("out_grouped%d" % lo, result, width))
-
-        for (base, end), grouped in zip(OUT_CHUNKS, out_grouped):
-            for lo, hi in pieces(base, end):
-                quantize(grouped, base, lo, hi, out_codes, out_scale)
-            nc.sync.dma_start(out=out_words[:, base:end], in_=out_codes[:, base:end])
+        for grouped, (lo, hi) in zip(out_grouped, OUT_PARTS):
+            quantize(grouped, lo, hi, out_codes, out_scale)
+            nc.sync.dma_start(out=words_of(out_1)[:, lo:hi], in_=out_codes[:, lo:hi])
         for q in range(4):
             queue = nc.sync if q % 2 == 0 else nc.scalar
             queue.dma_start(

@@ -17,13 +17,14 @@ COPY = mybir.ActivationFunctionType.Copy
 
 P = 128
 PACK = 4
+QUADRANTS = 4
 LIST_ROWS = 16
 H_SCALE = 0.0625
-SPLIT = 384
 HALF = S // 2
-Z_PARTS = ((0, SPLIT), (SPLIT, S))
-OUT_PARTS = ((0, HALF), (HALF, SPLIT), (SPLIT, S))
-QUANT_SPANS = ((0, HALF), (HALF, SPLIT), (SPLIT, S))
+LAST_PART = S - P
+Z_PARTS = ((0, LAST_PART), (LAST_PART, S))
+OUT_PARTS = ((0, HALF), (HALF, LAST_PART), (LAST_PART, S))
+QUANT_SPANS = ((0, HALF), (HALF, LAST_PART), (LAST_PART, S))
 
 
 def tile_picked_denseprodunder_none_po_kernel(
@@ -55,7 +56,7 @@ def tile_picked_denseprodunder_none_po_kernel(
         w_raw = sb("w_raw", [P, H], I32)
         w_scale_raw = sb("w_scale_raw", [P, H], U8)
         gain = sb("gain", [P, PACK], F32)
-        wide = [sb("wide%d" % i, [P, 2 * S], F32) for i in range(PACK)]
+        wide = [sb("wide%d" % i, [P, 2 * S], F32) for i in range(4)]
 
         nc.vector.memset(x_scale_table[:, 0 : T // 2].bitcast(I32), 0)
         nc.gpsimd.memset(x_scale_table[:, T // 2 : T].bitcast(I32), 0)
@@ -65,19 +66,20 @@ def tile_picked_denseprodunder_none_po_kernel(
             nc.vector.memset(window[:, S:], 0.0)
 
         def load_scale_rows(tile, dram):
-            for q in range(4):
+            for q in range(QUADRANTS):
                 nc.sync.dma_start(
                     out=tile[32 * q : 32 * q + 4, :].bitcast(I32), in_=dram[0, 4 * q : 4 * q + 4, :].bitcast(I32)
                 )
 
         nc.sync.dma_start(offs_t[:], offs)
+        nc.sync.dma_start(k1_t[:], k1)
         nc.sync.dma_start(out=x_table[:], in_=words_of(x_words))
         nc.sync.dma_start(out=w_raw[:], in_=words_of(w1_words))
         load_scale_rows(x_scale_table, x_scales)
         load_scale_rows(w_scale_raw, w1_scales)
         nc.gpsimd.dma_start(out=gain[:], in_=gs.rearrange("(p t) o -> p (t o)", t=PACK))
         nc.sync.dma_start(out=d_scale_table[0:P:8, :].bitcast(I32), in_=d_scales[0].bitcast(I32))
-        for tile, dram in ((k1_t, k1), (n1_t, n1), (n2_t, n2), (n3_t, n3), (n4_t, n4)):
+        for tile, dram in ((n1_t, n1), (n2_t, n2), (n3_t, n3), (n4_t, n4)):
             nc.sync.dma_start(tile[:], dram)
 
         def deal(dst, src):
@@ -111,7 +113,7 @@ def tile_picked_denseprodunder_none_po_kernel(
         y_gain = wide[0:2] + [sb("y_gain%d" % t, [P, S], F32) for t in (2, 3)]
         y_plain = wide[2:4] + [sb("y_plain%d" % t, [P, S], F32) for t in (2, 3)]
         for t in range(PACK):
-            bank = psum.tile([P, S], F32, name="y_bank%d" % t)
+            bank = psum.tile([P, S], F32, name="bank%d" % t)
             product(bank, w_codes, w_scale, t, x_codes, x_scale, 0, S)
             nc.scalar.activation(y_gain[t][:, 0:S], bank[:], COPY, scale=gain[:, t : t + 1])
             nc.scalar.activation(y_plain[t][:, 0:S], bank[:], COPY)
@@ -125,31 +127,31 @@ def tile_picked_denseprodunder_none_po_kernel(
         deal(d_scale_dealt, d_scale_picked)
         nc.vector.tensor_copy(d_picked[:].bitcast(U32), d_table[:].bitcast(U32).indirect(k1_t[:]))
         deal(d_codes, d_picked)
-        for q in range(4):
+        for q in range(QUADRANTS):
             nc.sync.dma_start(
                 out=d_scale[32 * q : 32 * q + 4, :].bitcast(I32),
                 in_=d_scale_dealt[32 * q : 32 * q + 32 : 8, :].bitcast(I32),
             )
 
-        def interleave(grouped, first_t, pair_columns):
-            nc.scalar.copy(out=grouped[:, :, first_t : first_t + 2], in_=pair_columns.rearrange("p t c -> p c t"))
-
-        def quantize(grouped, base, end, codes, scale):
-            for lo, hi in QUANT_SPANS:
-                if base <= lo and hi <= end:
-                    nc.vector.quantize_mx(
-                        out=codes[:, lo:hi].bitcast(FP8X4),
-                        scales=scale[:, lo:hi],
-                        in_=grouped[:, lo - base : hi - base, :].rearrange("p c t -> p (c t)"),
-                    )
-
         def steps(parts):
             return [(0, 0, S)] + [(2, lo, hi) for lo, hi in parts]
 
-        def interleave_step(grouped, parts, first_t, lo, hi, pair):
+        def group(grouped, parts, first_t, lo, hi, pair):
             for tile, (part_lo, part_hi) in zip(grouped, parts):
                 if lo <= part_lo and part_hi <= hi:
-                    interleave(tile, first_t, pair[:, :, part_lo - lo : part_hi - lo])
+                    nc.scalar.copy(
+                        out=tile[:, :, first_t : first_t + 2],
+                        in_=pair[:, :, part_lo - lo : part_hi - lo].rearrange("p t c -> p c t"),
+                    )
+
+        def quantize(tile, part_lo, part_hi, codes, scale):
+            for lo, hi in QUANT_SPANS:
+                if part_lo <= lo and hi <= part_hi:
+                    nc.vector.quantize_mx(
+                        out=codes[:, lo:hi].bitcast(FP8X4),
+                        scales=scale[:, lo:hi],
+                        in_=tile[:, lo - part_lo : hi - part_lo, :].rearrange("p c t -> p (c t)"),
+                    )
 
         z_grouped = [sb("z_grouped%d" % lo, [P, hi - lo, PACK], BF16) for lo, hi in Z_PARTS]
         for first_t, lo, hi in steps(Z_PARTS):
@@ -161,12 +163,12 @@ def tile_picked_denseprodunder_none_po_kernel(
                 nc.vector.tensor_tensor(
                     z[:, i, :], y_plain[first_t + i][:].indirect(entries(n2_t, lo, hi)), at_n1[:, i, :], ALU.mult
                 )
-            interleave_step(z_grouped, Z_PARTS, first_t, lo, hi, z)
+            group(z_grouped, Z_PARTS, first_t, lo, hi, z)
 
         z_codes = sb("z_codes", [P, S], I32)
         z_scale = sb("z_scale", [P, S], U8)
-        for grouped, (lo, hi) in zip(z_grouped, Z_PARTS):
-            quantize(grouped, lo, hi, z_codes, z_scale)
+        for tile, (lo, hi) in zip(z_grouped, Z_PARTS):
+            quantize(tile, lo, hi, z_codes, z_scale)
 
         h_neg = y_gain
         h = [sb("h%d" % t, [P, S], F32) for t in range(PACK)]
@@ -179,7 +181,7 @@ def tile_picked_denseprodunder_none_po_kernel(
         nc.vector.tensor_scalar(h_neg[0][:, HALF:S], right[:, HALF:S], -H_SCALE, None, ALU.mult)
         nc.scalar.activation(h[0][:, HALF:S], right[:, HALF:S], COPY, scale=H_SCALE)
         for t in range(1, PACK):
-            bank = psum.tile([P, S], F32, name="y_bank%d" % t)
+            bank = psum.tile([P, S], F32, name="bank%d" % t)
             product(bank, d_codes, d_scale, t, z_codes, z_scale, 0, S)
             nc.scalar.activation(h_neg[t][:, 0:S], bank[:], COPY, scale=-H_SCALE)
             nc.scalar.activation(h[t][:], bank[:], COPY, scale=H_SCALE)
@@ -187,34 +189,37 @@ def tile_picked_denseprodunder_none_po_kernel(
         out_rows = out_0.rearrange("(p t) j -> p t j", t=PACK)
         out_grouped = [sb("out_grouped%d" % lo, [P, hi - lo, PACK], BF16) for lo, hi in OUT_PARTS]
 
-        def above(dst, t, list_tile, lo, hi):
+        def difference(dst, t, list_tile, lo, hi):
             nc.vector.tensor_tensor(dst, h_neg[t][:].indirect(entries(list_tile, lo, hi)), h[t][:, lo:hi], ALU.add)
 
-        def finish(first_t, lo, hi, above3, above4):
+        def finish(first_t, lo, hi, less_n3, less_n4):
             result = sb("result_%d_%d" % (first_t, lo), [P, 2, hi - lo], F32)
-            nc.vector.tensor_tensor(result[:], above3[:], above4[:], ALU.max)
+            nc.vector.tensor_tensor(result[:], less_n3[:], less_n4[:], ALU.max)
             nc.sync.dma_start(out=out_rows[:, first_t : first_t + 2, lo:hi], in_=result[:])
-            interleave_step(out_grouped, OUT_PARTS, first_t, lo, hi, result)
+            group(out_grouped, OUT_PARTS, first_t, lo, hi, result)
 
         pending = None
         for first_t, lo, hi in steps(OUT_PARTS):
-            above3 = sb("above3_%d_%d" % (first_t, lo), [P, 2, hi - lo], F32)
-            above4 = sb("above4_%d_%d" % (first_t, lo), [P, 2, hi - lo], F32)
-            above(above3[:, 0, :], first_t, n3_t, lo, hi)
+            less_n3 = sb("less_n3_%d_%d" % (first_t, lo), [P, 2, hi - lo], F32)
+            less_n4 = sb("less_n4_%d_%d" % (first_t, lo), [P, 2, hi - lo], F32)
             if pending:
+                difference(less_n3[:, 0, :], first_t, n3_t, lo, hi)
                 finish(*pending)
-            above(above4[:, 0, :], first_t, n4_t, lo, hi)
-            above(above3[:, 1, :], first_t + 1, n3_t, lo, hi)
-            above(above4[:, 1, :], first_t + 1, n4_t, lo, hi)
-            pending = (first_t, lo, hi, above3, above4)
+            else:
+                difference(less_n3[:, 0, 0:HALF], first_t, n3_t, 0, HALF)
+                difference(less_n3[:, 0, HALF:S], first_t, n3_t, HALF, S)
+            difference(less_n4[:, 0, :], first_t, n4_t, lo, hi)
+            difference(less_n3[:, 1, :], first_t + 1, n3_t, lo, hi)
+            difference(less_n4[:, 1, :], first_t + 1, n4_t, lo, hi)
+            pending = (first_t, lo, hi, less_n3, less_n4)
         finish(*pending)
 
         out_codes = sb("out_codes", [P, S], I32)
         out_scale = sb("out_scale", [P, S], U8)
-        for grouped, (lo, hi) in zip(out_grouped, OUT_PARTS):
-            quantize(grouped, lo, hi, out_codes, out_scale)
+        for tile, (lo, hi) in zip(out_grouped, OUT_PARTS):
+            quantize(tile, lo, hi, out_codes, out_scale)
             nc.sync.dma_start(out=words_of(out_1)[:, lo:hi], in_=out_codes[:, lo:hi])
-        for q in range(4):
+        for q in range(QUADRANTS):
             queue = nc.sync if q % 2 == 0 else nc.scalar
             queue.dma_start(
                 out=out_2[0, 4 * q : 4 * q + 4, :].bitcast(I32), in_=out_scale[32 * q : 32 * q + 4, :].bitcast(I32)

from contextlib import ExitStack

import concourse.mybir as mybir

T, S, H, G = 2048, 512, 512, 2048
FLOPS = 2 * 2 * 512 * 512 * 512

F32 = mybir.dt.float32
BF16 = mybir.dt.bfloat16
I32 = mybir.dt.int32
U32 = mybir.dt.uint32
U16 = mybir.dt.uint16
U8 = mybir.dt.uint8
FP8X4 = mybir.dt.float8_e4m3fn_x4
ALU = mybir.AluOpType
COPY = mybir.ActivationFunctionType.Copy

P = 128
PACK = 4
QUADRANTS = 4
LIST_ROWS = 16
H_SCALE = 0.0625
HALF = S // 2
LAST_PART = S - P
Z_PARTS = ((0, LAST_PART), (LAST_PART, S))
OUT_PARTS = ((0, HALF), (HALF, LAST_PART), (LAST_PART, S))
QUANT_SPANS = ((0, HALF), (HALF, LAST_PART), (LAST_PART, S))


def tile_picked_denseprodunder_none_po_kernel(
    tc, x_words, x_scales, w1_words, w1_scales, gs, d_words, d_scales, offs, n1, n2, k1, n3, n4, out_0, out_1, out_2
):
    nc = tc.nc

    def words_of(dram):
        return dram[0].rearrange("p n t -> p (n t)").bitcast(I32)

    def entries(list_tile, lo, hi):
        return list_tile[:, lo // LIST_ROWS : hi // LIST_ROWS]

    with ExitStack() as ctx:
        lists = ctx.enter_context(tc.tile_pool(name="lists", bufs=1))
        pool = ctx.enter_context(tc.tile_pool(name="pool", bufs=1))
        psum = ctx.enter_context(tc.psum_pool(name="psum", bufs=1))

        def sb(name, shape, dtype, tag=None):
            return pool.tile(shape, dtype, name=name, tag=tag or name, align_bytes=64)

        offs_t, k1_t, n1_t, n2_t, n3_t, n4_t = [
            lists.tile([P, S // LIST_ROWS], U16, name=name) for name in ("offs_t", "k1_t", "n1_t", "n2_t", "n3_t", "n4_t")
        ]

        x_table = sb("x_table", [P, T], I32)
        x_scale_table = sb("x_scale_table", [P, T], U8)
        d_scale_table = sb("d_scale_table", [P, G], U8)
        w_raw = sb("w_raw", [P, H], I32)
        w_scale_raw = sb("w_scale_raw", [P, H], U8)
        gain = sb("gain", [P, PACK], F32)
        wide = [sb("wide%d" % i, [P, 2 * S], F32) for i in range(4)]

        nc.vector.memset(x_scale_table[:, 0 : T // 2].bitcast(I32), 0)
        nc.gpsimd.memset(x_scale_table[:, T // 2 : T].bitcast(I32), 0)
        nc.vector.memset(w_scale_raw[:].bitcast(I32), 0)
        nc.vector.memset(d_scale_table[:].bitcast(I32), 0)
        for window in wide:
            nc.vector.memset(window[:, S:], 0.0)

        def load_scale_rows(tile, dram):
            for q in range(QUADRANTS):
                nc.sync.dma_start(
                    out=tile[32 * q : 32 * q + 4, :].bitcast(I32), in_=dram[0, 4 * q : 4 * q + 4, :].bitcast(I32)
                )

        nc.sync.dma_start(offs_t[:], offs)
        nc.sync.dma_start(k1_t[:], k1)
        nc.sync.dma_start(out=x_table[:], in_=words_of(x_words))
        nc.sync.dma_start(out=w_raw[:], in_=words_of(w1_words))
        load_scale_rows(x_scale_table, x_scales)
        load_scale_rows(w_scale_raw, w1_scales)
        nc.gpsimd.dma_start(out=gain[:], in_=gs.rearrange("(p t) o -> p (t o)", t=PACK))
        nc.sync.dma_start(out=d_scale_table[0:P:8, :].bitcast(I32), in_=d_scales[0].bitcast(I32))
        for tile, dram in ((n1_t, n1), (n2_t, n2), (n3_t, n3), (n4_t, n4)):
            nc.sync.dma_start(tile[:], dram)

        def deal(dst, src):
            nc.vector.tensor_copy(
                out=dst[:].rearrange("p (t m) -> p m t", t=PACK), in_=src[:].rearrange("p (m t) -> p m t", t=PACK)
            )

        x_scale = sb("x_scale", [P, S], U8)
        x_codes = sb("x_codes", [P, S], I32)
        w_codes = sb("w_codes", [P, H], I32)
        w_scale = sb("w_scale", [P, H], U8)
        nc.vector.tensor_copy(x_scale[:], x_scale_table[:].indirect(offs_t[:]))
        d_table = sb("d_table", [P, G], I32, tag="x_scale_table")
        nc.sync.dma_start(out=d_table[:], in_=words_of(d_words))
        nc.vector.tensor_copy(x_codes[:].bitcast(U32), x_table[:].bitcast(U32).indirect(offs_t[:]))
        deal(w_codes, w_raw)
        deal(w_scale, w_scale_raw)

        def product(bank, codes, scale, t, moving, moving_scale, lo, hi):
            cols = slice(t * P, (t + 1) * P)
            nc.tensor.matmul_mx(
                out=bank[:, lo:hi],
                lhsT=codes[:, cols].bitcast(FP8X4),
                lhsT_scale=scale[:, cols],
                rhs=moving[:, lo:hi].bitcast(FP8X4),
                rhs_scale=moving_scale[:, lo:hi],
                start=True,
                stop=True,
            )

        y_gain = wide[0:2] + [sb("y_gain%d" % t, [P, S], F32) for t in (2, 3)]
        y_plain = wide[2:4] + [sb("y_plain%d" % t, [P, S], F32) for t in (2, 3)]
        for t in range(PACK):
            bank = psum.tile([P, S], F32, name="bank%d" % t)
            product(bank, w_codes, w_scale, t, x_codes, x_scale, 0, S)
            nc.scalar.activation(y_gain[t][:, 0:S], bank[:], COPY, scale=gain[:, t : t + 1])
            nc.scalar.activation(y_plain[t][:, 0:S], bank[:], COPY)

        d_scale_picked = sb("d_scale_picked", [P, H], U8, tag="w_scale_raw")
        d_scale_dealt = sb("d_scale_dealt", [P, H], U8)
        d_scale = sb("d_scale", [P, H], U8)
        d_picked = sb("d_picked", [P, H], I32)
        d_codes = sb("d_codes", [P, H], I32)
        nc.vector.tensor_copy(d_scale_picked[:], d_scale_table[:].indirect(k1_t[:]))
        deal(d_scale_dealt, d_scale_picked)
        nc.vector.tensor_copy(d_picked[:].bitcast(U32), d_table[:].bitcast(U32).indirect(k1_t[:]))
        deal(d_codes, d_picked)
        for q in range(QUADRANTS):
            nc.sync.dma_start(
                out=d_scale[32 * q : 32 * q + 4, :].bitcast(I32),
                in_=d_scale_dealt[32 * q : 32 * q + 32 : 8, :].bitcast(I32),
            )

        def steps(parts):
            return [(0, 0, S)] + [(2, lo, hi) for lo, hi in parts]

        def group(grouped, parts, first_t, lo, hi, pair):
            for tile, (part_lo, part_hi) in zip(grouped, parts):
                if lo <= part_lo and part_hi <= hi:
                    nc.scalar.copy(
                        out=tile[:, :, first_t : first_t + 2],
                        in_=pair[:, :, part_lo - lo : part_hi - lo].rearrange("p t c -> p c t"),
                    )

        def quantize(tile, part_lo, part_hi, codes, scale):
            for lo, hi in QUANT_SPANS:
                if part_lo <= lo and hi <= part_hi:
                    nc.vector.quantize_mx(
                        out=codes[:, lo:hi].bitcast(FP8X4),
                        scales=scale[:, lo:hi],
                        in_=tile[:, lo - part_lo : hi - part_lo, :].rearrange("p c t -> p (c t)"),
                    )

        z_grouped = [sb("z_grouped%d" % lo, [P, hi - lo, PACK], BF16) for lo, hi in Z_PARTS]
        for first_t, lo, hi in steps(Z_PARTS):
            at_n1 = sb("at_n1_%d_%d" % (first_t, lo), [P, 2, hi - lo], F32)
            z = sb("z_%d_%d" % (first_t, lo), [P, 2, hi - lo], F32)
            for i in range(2):
                nc.vector.tensor_copy(at_n1[:, i, :], y_gain[first_t + i][:].indirect(entries(n1_t, lo, hi)))
            for i in range(2):
                nc.vector.tensor_tensor(
                    z[:, i, :], y_plain[first_t + i][:].indirect(entries(n2_t, lo, hi)), at_n1[:, i, :], ALU.mult
                )
            group(z_grouped, Z_PARTS, first_t, lo, hi, z)

        z_codes = sb("z_codes", [P, S], I32)
        z_scale = sb("z_scale", [P, S], U8)
        for tile, (lo, hi) in zip(z_grouped, Z_PARTS):
            quantize(tile, lo, hi, z_codes, z_scale)

        h_neg = y_gain
        h = [sb("h%d" % t, [P, S], F32) for t in range(PACK)]
        left = psum.tile([P, S], F32, name="h_left")
        right = psum.tile([P, S], F32, name="h_right")
        product(left, d_codes, d_scale, 0, z_codes, z_scale, 0, HALF)
        product(right, d_codes, d_scale, 0, z_codes, z_scale, HALF, S)
        nc.scalar.activation(h_neg[0][:, 0:HALF], left[:, 0:HALF], COPY, scale=-H_SCALE)
        nc.scalar.activation(h[0][:, 0:HALF], left[:, 0:HALF], COPY, scale=H_SCALE)
        nc.vector.tensor_scalar(h_neg[0][:, HALF:S], right[:, HALF:S], -H_SCALE, None, ALU.mult)
        nc.scalar.activation(h[0][:, HALF:S], right[:, HALF:S], COPY, scale=H_SCALE)
        for t in range(1, PACK):
            bank = psum.tile([P, S], F32, name="bank%d" % t)
            product(bank, d_codes, d_scale, t, z_codes, z_scale, 0, S)
            nc.scalar.activation(h_neg[t][:, 0:S], bank[:], COPY, scale=-H_SCALE)
            nc.scalar.activation(h[t][:], bank[:], COPY, scale=H_SCALE)

        out_rows = out_0.rearrange("(p t) j -> p t j", t=PACK)
        out_grouped = [sb("out_grouped%d" % lo, [P, hi - lo, PACK], BF16) for lo, hi in OUT_PARTS]

        def difference(dst, t, list_tile, lo, hi):
            nc.vector.tensor_tensor(dst, h_neg[t][:].indirect(entries(list_tile, lo, hi)), h[t][:, lo:hi], ALU.add)

        def finish(first_t, lo, hi, less_n3, less_n4):
            result = sb("result_%d_%d" % (first_t, lo), [P, 2, hi - lo], F32)
            nc.vector.tensor_tensor(result[:], less_n3[:], less_n4[:], ALU.max)
            nc.sync.dma_start(out=out_rows[:, first_t : first_t + 2, lo:hi], in_=result[:])
            group(out_grouped, OUT_PARTS, first_t, lo, hi, result)

        pending = None
        for first_t, lo, hi in steps(OUT_PARTS):
            less_n3 = sb("less_n3_%d_%d" % (first_t, lo), [P, 2, hi - lo], F32)
            less_n4 = sb("less_n4_%d_%d" % (first_t, lo), [P, 2, hi - lo], F32)
            if pending:
                difference(less_n3[:, 0, :], first_t, n3_t, lo, hi)
                finish(*pending)
            else:
                difference(less_n3[:, 0, 0:HALF], first_t, n3_t, 0, HALF)
                difference(less_n3[:, 0, HALF:S], first_t, n3_t, HALF, S)
            difference(less_n4[:, 0, :], first_t, n4_t, lo, hi)
            difference(less_n3[:, 1, :], first_t + 1, n3_t, lo, hi)
            difference(less_n4[:, 1, :], first_t + 1, n4_t, lo, hi)
            pending = (first_t, lo, hi, less_n3, less_n4)
        finish(*pending)

        out_codes = sb("out_codes", [P, S], I32)
        out_scale = sb("out_scale", [P, S], U8)
        for tile, (lo, hi) in zip(out_grouped, OUT_PARTS):
            quantize(tile, lo, hi, out_codes, out_scale)
            nc.sync.dma_start(out=words_of(out_1)[:, lo:hi], in_=out_codes[:, lo:hi])
        for q in range(QUADRANTS):
            queue = nc.sync if q % 2 == 0 else nc.scalar
            queue.dma_start(
                out=out_2[0, 4 * q : 4 * q + 4, :].bitcast(I32), in_=out_scale[32 * q : 32 * q + 4, :].bitcast(I32)
            )
